import numpy as np
import ml_dtypes


def mxq(x, axis, fmt="e4m3"):
    dtype, down = {"e4m3": (ml_dtypes.float8_e4m3fn, 7), "e5m2": (ml_dtypes.float8_e5m2, 14)}[fmt]
    v = np.moveaxis(np.asarray(x, np.float32).astype(ml_dtypes.bfloat16).astype(np.float64), axis, -1)
    blocks = v.reshape(v.shape[:-1] + (-1, 32))
    amax = np.abs(blocks).max(-1, keepdims=True)
    byte = np.maximum(np.where(amax > 0, np.frexp(amax)[1] - 1 + 127, 0) - down, 1)
    scale = np.exp2(byte - 127.0)
    codes = (blocks / scale).astype(np.float32).astype(dtype).astype(np.float64)
    return np.moveaxis((codes * scale).reshape(v.shape), -1, axis)


WIDE = False


def mx_kscale(k):
    if not WIDE:
        return np.ones(k)
    levels = np.array([10, -10, 5, -5, 0])
    if k % 512:
        return np.exp2(np.random.permutation(np.resize(levels, k // 32))).repeat(32)
    a = np.empty((k // 512, 16))
    for p in range(k // 512):
        a[p, :8] = np.random.permutation(np.resize(levels, 8))
        for g in range(8):
            far = levels[np.abs(levels - a[p, g]) >= 10]
            a[p, g + 8] = far[np.random.randint(len(far))]
    return np.exp2(a.ravel()).repeat(32)


def f64(x):
    return np.asarray(x).astype(np.float64)


def striped(idx):
    return np.tile(idx.reshape(-1, 16).T, (8, 1)).astype(np.uint16)


def unstriped(offs):
    return offs[:16].T.reshape(-1).astype(np.int64)


def pack_weight(w):
    k, n = w.shape
    w = f64(np.asarray(w, np.float32).astype(ml_dtypes.bfloat16)).reshape(k // 32, 32, n)
    amax = np.abs(w).max(1)
    byte = np.clip(np.where(amax > 0, np.frexp(amax)[1] - 1 + 127 - 7, 1), 1, 254)
    scaled = (w * np.exp2(127.0 - byte)[:, None, :]).reshape(k, n).astype(np.float32)
    words = np.ascontiguousarray(scaled.reshape(k // 512, 128, 4, n).transpose(0, 1, 3, 2)).astype(ml_dtypes.float8_e4m3fn).view(np.uint8)
    return words, np.ascontiguousarray(byte.astype(np.uint8).reshape(k // 512, 16, n))


def unpack_weight(words, scales):
    g, p, n, _ = words.shape
    vals = np.ascontiguousarray(words).view(ml_dtypes.float8_e4m3fn).astype(np.float64) * np.repeat(np.exp2(scales.astype(np.float64) - 127.0), 8, axis=1)[..., None]
    return vals.transpose(0, 1, 3, 2).reshape(g * 512, n)


def sigmoid(v):
    return 1.0 / (1.0 + np.exp(-np.maximum(v, -700.0)))


K, T, S, N, U = 512, 1024, 512, 256, 1024


def setup_inputs():
    n = np.random.standard_normal
    s = mx_kscale(K)[:, None]
    packed_w1 = pack_weight(n((K, N)) / np.sqrt(K) / s)
    return {
        "xT": (n((K, T)) * s).astype(np.float32),
        "mem": n((N, U)).astype(np.float32),
        "w1_words": packed_w1[0],
        "w1_scales": packed_w1[1],
        "offs": striped(np.random.permutation(T)[:S]),
        "slot": striped(np.random.permutation(U)[:S]),
    }


def reference(xT, mem, w1_words, w1_scales, offs, slot):
    xq = mxq(f64(xT)[:, unstriped(offs)], 0, "e4m3")
    y = unpack_weight(w1_words, w1_scales).T @ xq
    out = f64(mem).copy()
    out[:, unstriped(slot)] = f64(mem)[:, unstriped(slot)] * sigmoid(y)
    return out

@@ -1,0 +1,103 @@
+from contextlib import ExitStack
+
+import concourse.mybir as mybir
+
+K, T, S, N, U = 512, 1024, 512, 256, 1024
+FLOPS = 2 * K * N * S
+
+F32 = mybir.dt.float32
+BF16 = mybir.dt.bfloat16
+I32 = mybir.dt.int32
+U32 = mybir.dt.uint32
+U16 = mybir.dt.uint16
+U8 = mybir.dt.uint8
+FP8X4 = mybir.dt.float8_e4m3fn_x4
+SIGMOID = mybir.ActivationFunctionType.Sigmoid
+MULT = mybir.AluOpType.mult
+
+P = 128
+PACK = 4
+HALF = S // 2
+LIST_COLS = S // 16
+
+
+def tile_picked_idxput_gate_e_kernel(tc, xT, mem, w1_words, w1_scales, offs, slot, out):
+    nc = tc.nc
+    with ExitStack() as ctx:
+        keep = ctx.enter_context(tc.tile_pool(name="keep", bufs=1))
+        psum = ctx.enter_context(tc.psum_pool(name="psum", bufs=1))
+
+        offs_sb = keep.tile([P, LIST_COLS], U16, name="offs_sb")
+        slot_sb = keep.tile([P, LIST_COLS], U16, name="slot_sb")
+        planes = [keep.tile([P, T], F32, name="plane%d" % t) for t in range(PACK)]
+        store = [keep.tile([P, U], F32, name="store%d" % b) for b in range(2)]
+        w_words = keep.tile([P, N], U32, name="w_words", align_bytes=64)
+        w_scales = keep.tile([P, N], U8, name="w_scales", align_bytes=64)
+
+        x_rows = xT.rearrange("(p t) c -> p t c", t=PACK)
+        nc.sync.dma_start(planes[0][:], x_rows[:, 0, :])
+        nc.sync.dma_start(offs_sb[:], offs)
+        for t in range(1, PACK):
+            nc.sync.dma_start(planes[t][:], x_rows[:, t, :])
+        nc.sync.dma_start(slot_sb[:], slot)
+        nc.sync.dma_start(store[0][:], mem[0:P, :])
+        nc.sync.dma_start(w_words[:].bitcast(I32), w1_words[0].rearrange("p n t -> p (n t)").bitcast(I32))
+        nc.sync.dma_start(store[1][:], mem[P : 2 * P, :])
+
+        nc.gpsimd.memset(w_scales[:].bitcast(I32), 0)
+        for q in range(4):
+            nc.gpsimd.dma_start(w_scales[32 * q : 32 * q + 4, :].bitcast(I32), w1_scales[0, 4 * q : 4 * q + 4, :].bitcast(I32))
+
+        warm = keep.tile([P, 2], F32, name="warm")
+        nc.vector.memset(warm[:, 0:1], 0.0)
+        nc.scalar.activation(warm[:, 1:2], warm[:, 0:1], SIGMOID)
+
+        def half_cols(h):
+            return slice(h * HALF, (h + 1) * HALF)
+
+        def half_list(tile, h):
+            return tile[:, h * LIST_COLS // 2 : (h + 1) * LIST_COLS // 2]
+
+        picked = keep.tile([P, PACK, S], BF16, name="picked")
+        for t in range(PACK - 1):
+            nc.vector.tensor_copy(picked[:, t, :], planes[t][:].indirect(offs_sb[:]))
+        for h in range(2):
+            nc.vector.tensor_copy(picked[:, PACK - 1, half_cols(h)], planes[PACK - 1][:].indirect(half_list(offs_sb, h)))
+
+        grouped = [keep.tile([P, HALF, PACK], BF16, name="grouped%d" % h, align_bytes=64) for h in range(2)]
+        codes = [keep.tile([P, HALF], U32, name="codes%d" % h, align_bytes=64) for h in range(2)]
+        scales = [keep.tile([P, HALF], U8, name="scales%d" % h, align_bytes=64) for h in range(2)]
+        old = [keep.tile([P, S], F32, name="old%d" % b) for b in range(2)]
+        gate = [keep.tile([P, S], F32, name="gate%d" % b) for b in range(2)]
+        acc = [[psum.tile([P, HALF], F32, name="acc%d_%d" % (b, h)) for h in range(2)] for b in range(2)]
+
+        for h in range(2):
+            nc.scalar.copy(
+                grouped[h][:].rearrange("p (c i) t -> p c t i", i=4),
+                picked[:, :, half_cols(h)].rearrange("p t (c i) -> p c t i", i=4),
+            )
+        for h in range(2):
+            nc.vector.tensor_copy(old[h][:], store[h][:].indirect(slot_sb[:]))
+            nc.vector.quantize_mx(
+                out=codes[h][:].bitcast(FP8X4), scales=scales[h][:], in_=grouped[h][:].rearrange("p n t -> p (n t)")
+            )
+            for b in range(2):
+                nc.tensor.matmul_mx(
+                    out=acc[b][h][:],
+                    lhsT=w_words[:, b * P : (b + 1) * P].bitcast(FP8X4),
+                    lhsT_scale=w_scales[:, b * P : (b + 1) * P],
+                    rhs=codes[h][:].bitcast(FP8X4),
+                    rhs_scale=scales[h][:],
+                    start=True,
+                    stop=True,
+                )
+        for b in range(2):
+            for h in range(2):
+                nc.scalar.activation(gate[b][:, half_cols(h)], acc[b][h][:], SIGMOID)
+        for h in range(2):
+            nc.vector.tensor_tensor(
+                store[0][:].indirect(half_list(slot_sb, h)), old[0][:, half_cols(h)], gate[0][:, half_cols(h)], MULT
+            )
+        nc.sync.dma_start(out[0:P, :], store[0][:])
+        nc.vector.tensor_tensor(store[1][:].indirect(slot_sb[:]), old[1][:], gate[1][:], MULT)
+        nc.sync.dma_start(out[P : 2 * P, :], store[1][:])

@@ -13,11 +13,13 @@ U16 = mybir.dt.uint16
 U8 = mybir.dt.uint8
 FP8X4 = mybir.dt.float8_e4m3fn_x4
 SIGMOID = mybir.ActivationFunctionType.Sigmoid
+COPY = mybir.ActivationFunctionType.Copy
 MULT = mybir.AluOpType.mult
 
 P = 128
 PACK = 4
 HALF = S // 2
+SPLIT = 384
 LIST_COLS = S // 16
 
 
@@ -35,18 +37,19 @@ def tile_picked_idxput_gate_e_kernel(tc, xT, mem, w1_words, w1_scales, offs, slo
         w_scales = keep.tile([P, N], U8, name="w_scales", align_bytes=64)
 
         x_rows = xT.rearrange("(p t) c -> p t c", t=PACK)
-        nc.sync.dma_start(planes[0][:], x_rows[:, 0, :])
+        nc.sync.dma_start(planes[2][:], x_rows[:, 2, :])
         nc.sync.dma_start(offs_sb[:], offs)
-        for t in range(1, PACK):
+        for t in (0, 1):
             nc.sync.dma_start(planes[t][:], x_rows[:, t, :])
         nc.sync.dma_start(slot_sb[:], slot)
         nc.sync.dma_start(store[0][:], mem[0:P, :])
-        nc.sync.dma_start(w_words[:].bitcast(I32), w1_words[0].rearrange("p n t -> p (n t)").bitcast(I32))
+        nc.sync.dma_start(planes[3][:], x_rows[:, 3, :])
         nc.sync.dma_start(store[1][:], mem[P : 2 * P, :])
+        nc.sync.dma_start(w_words[:].bitcast(I32), w1_words[0].rearrange("p n t -> p (n t)").bitcast(I32))
 
-        nc.gpsimd.memset(w_scales[:].bitcast(I32), 0)
+        nc.vector.memset(w_scales[:].bitcast(I32), 0)
         for q in range(4):
-            nc.gpsimd.dma_start(w_scales[32 * q : 32 * q + 4, :].bitcast(I32), w1_scales[0, 4 * q : 4 * q + 4, :].bitcast(I32))
+            nc.sync.dma_start(w_scales[32 * q : 32 * q + 4, :].bitcast(I32), w1_scales[0, 4 * q : 4 * q + 4, :].bitcast(I32))
 
         warm = keep.tile([P, 2], F32, name="warm")
         nc.vector.memset(warm[:, 0:1], 0.0)
@@ -58,46 +61,59 @@ def tile_picked_idxput_gate_e_kernel(tc, xT, mem, w1_words, w1_scales, offs, slo
         def half_list(tile, h):
             return tile[:, h * LIST_COLS // 2 : (h + 1) * LIST_COLS // 2]
 
-        picked = keep.tile([P, PACK, S], BF16, name="picked")
-        for t in range(PACK - 1):
+        old = [keep.tile([P, S], F32, name="old%d" % b) for b in range(2)]
+        grouped = keep.tile([P, S, PACK], BF16, name="grouped", align_bytes=64)
+        picked = keep.tile([P, 2, S], BF16, name="picked")
+
+        def gather_shared(t, cuts):
+            for lo, hi in zip(cuts, cuts[1:]):
+                nc.vector.tensor_copy(grouped[:, lo:hi, t], planes[t][:].indirect(offs_sb[:, lo // 16 : hi // 16]))
+            rounded = keep.tile([P, T], BF16, name="rounded%d" % t)
+            nc.scalar.copy(rounded[:], planes[t][:])
+            nc.scalar.activation(grouped[:, SPLIT:S, t], rounded[:].indirect(offs_sb[:, SPLIT // 16 : S // 16]), COPY)
+
+        gather_shared(2, (0, SPLIT))
+        for t in range(2):
             nc.vector.tensor_copy(picked[:, t, :], planes[t][:].indirect(offs_sb[:]))
         for h in range(2):
-            nc.vector.tensor_copy(picked[:, PACK - 1, half_cols(h)], planes[PACK - 1][:].indirect(half_list(offs_sb, h)))
+            nc.scalar.copy(grouped[:, half_cols(h), 0:2], picked[:, :, half_cols(h)].rearrange("p t n -> p n t"))
+        nc.vector.tensor_copy(old[0][:], store[0][:].indirect(slot_sb[:]))
+        gather_shared(3, (0, HALF, SPLIT))
 
-        grouped = [keep.tile([P, HALF, PACK], BF16, name="grouped%d" % h, align_bytes=64) for h in range(2)]
-        codes = [keep.tile([P, HALF], U32, name="codes%d" % h, align_bytes=64) for h in range(2)]
-        scales = [keep.tile([P, HALF], U8, name="scales%d" % h, align_bytes=64) for h in range(2)]
-        old = [keep.tile([P, S], F32, name="old%d" % b) for b in range(2)]
+        codes = keep.tile([P, S], U32, name="codes", align_bytes=64)
+        scales = keep.tile([P, S], U8, name="scales", align_bytes=64)
         gate = [keep.tile([P, S], F32, name="gate%d" % b) for b in range(2)]
         acc = [[psum.tile([P, HALF], F32, name="acc%d_%d" % (b, h)) for h in range(2)] for b in range(2)]
 
-        for h in range(2):
-            nc.scalar.copy(
-                grouped[h][:].rearrange("p (c i) t -> p c t i", i=4),
-                picked[:, :, half_cols(h)].rearrange("p t (c i) -> p c t i", i=4),
-            )
-        for h in range(2):
-            nc.vector.tensor_copy(old[h][:], store[h][:].indirect(slot_sb[:]))
+        def gates(h):
+            cols = half_cols(h)
             nc.vector.quantize_mx(
-                out=codes[h][:].bitcast(FP8X4), scales=scales[h][:], in_=grouped[h][:].rearrange("p n t -> p (n t)")
+                out=codes[:, cols].bitcast(FP8X4),
+                scales=scales[:, cols],
+                in_=grouped[:, cols, :].rearrange("p n t -> p (n t)"),
             )
             for b in range(2):
                 nc.tensor.matmul_mx(
                     out=acc[b][h][:],
                     lhsT=w_words[:, b * P : (b + 1) * P].bitcast(FP8X4),
                     lhsT_scale=w_scales[:, b * P : (b + 1) * P],
-                    rhs=codes[h][:].bitcast(FP8X4),
-                    rhs_scale=scales[h][:],
+                    rhs=codes[:, cols].bitcast(FP8X4),
+                    rhs_scale=scales[:, cols],
                     start=True,
                     stop=True,
                 )
-        for b in range(2):
-            for h in range(2):
-                nc.scalar.activation(gate[b][:, half_cols(h)], acc[b][h][:], SIGMOID)
-        for h in range(2):
+                nc.scalar.activation(gate[b][:, cols], acc[b][h][:], SIGMOID)
+
+        def put(b, h):
             nc.vector.tensor_tensor(
-                store[0][:].indirect(half_list(slot_sb, h)), old[0][:, half_cols(h)], gate[0][:, half_cols(h)], MULT
+                store[b][:].indirect(half_list(slot_sb, h)), old[b][:, half_cols(h)], gate[b][:, half_cols(h)], MULT
             )
-        nc.sync.dma_start(out[0:P, :], store[0][:])
-        nc.vector.tensor_tensor(store[1][:].indirect(slot_sb[:]), old[1][:], gate[1][:], MULT)
-        nc.sync.dma_start(out[P : 2 * P, :], store[1][:])
+
+        gates(0)
+        nc.vector.tensor_copy(old[1][:], store[1][:].indirect(slot_sb[:]))
+        put(0, 0)
+        gates(1)
+        put(1, 0)
+        for b in range(2):
+            put(b, 1)
+            nc.sync.dma_start(out[b * P : (b + 1) * P, :], store[b][:])

@@ -19,7 +19,8 @@ MULT = mybir.AluOpType.mult
 P = 128
 PACK = 4
 HALF = S // 2
-SPLIT = 384
+SPLIT = 256
+FIRST = 128
 LIST_COLS = S // 16
 
 
@@ -37,19 +38,20 @@ def tile_picked_idxput_gate_e_kernel(tc, xT, mem, w1_words, w1_scales, offs, slo
         w_scales = keep.tile([P, N], U8, name="w_scales", align_bytes=64)
 
         x_rows = xT.rearrange("(p t) c -> p t c", t=PACK)
+        w_rows = w1_words[0].rearrange("p n t -> p (n t)").bitcast(I32)
+        nc.vector.memset(w_scales[:].bitcast(I32), 0)
         nc.sync.dma_start(planes[2][:], x_rows[:, 2, :])
         nc.sync.dma_start(offs_sb[:], offs)
-        for t in (0, 1):
-            nc.sync.dma_start(planes[t][:], x_rows[:, t, :])
-        nc.sync.dma_start(slot_sb[:], slot)
-        nc.sync.dma_start(store[0][:], mem[0:P, :])
-        nc.sync.dma_start(planes[3][:], x_rows[:, 3, :])
-        nc.sync.dma_start(store[1][:], mem[P : 2 * P, :])
-        nc.sync.dma_start(w_words[:].bitcast(I32), w1_words[0].rearrange("p n t -> p (n t)").bitcast(I32))
-
-        nc.vector.memset(w_scales[:].bitcast(I32), 0)
+        nc.sync.dma_start(planes[0][:], x_rows[:, 0, :])
         for q in range(4):
             nc.sync.dma_start(w_scales[32 * q : 32 * q + 4, :].bitcast(I32), w1_scales[0, 4 * q : 4 * q + 4, :].bitcast(I32))
+        nc.sync.dma_start(planes[1][:], x_rows[:, 1, :])
+        nc.sync.dma_start(slot_sb[:], slot)
+        nc.sync.dma_start(store[0][:], mem[0:P, :])
+        nc.sync.dma_start(w_words[:, 0:P].bitcast(I32), w_rows[:, 0:P])
+        nc.sync.dma_start(planes[3][:], x_rows[:, 3, :])
+        nc.sync.dma_start(store[1][:], mem[P : 2 * P, :])
+        nc.sync.dma_start(w_words[:, P : 2 * P].bitcast(I32), w_rows[:, P : 2 * P])
 
         warm = keep.tile([P, 2], F32, name="warm")
         nc.vector.memset(warm[:, 0:1], 0.0)
@@ -65,55 +67,68 @@ def tile_picked_idxput_gate_e_kernel(tc, xT, mem, w1_words, w1_scales, offs, slo
         grouped = keep.tile([P, S, PACK], BF16, name="grouped", align_bytes=64)
         picked = keep.tile([P, 2, S], BF16, name="picked")
 
-        def gather_shared(t, cuts):
+        rounded = {t: keep.tile([P, T], BF16, name="rounded%d" % t) for t in (2, 3)}
+
+        def gather_vector(t, cuts):
             for lo, hi in zip(cuts, cuts[1:]):
                 nc.vector.tensor_copy(grouped[:, lo:hi, t], planes[t][:].indirect(offs_sb[:, lo // 16 : hi // 16]))
-            rounded = keep.tile([P, T], BF16, name="rounded%d" % t)
-            nc.scalar.copy(rounded[:], planes[t][:])
-            nc.scalar.activation(grouped[:, SPLIT:S, t], rounded[:].indirect(offs_sb[:, SPLIT // 16 : S // 16]), COPY)
+            nc.scalar.copy(rounded[t][:], planes[t][:])
 
-        gather_shared(2, (0, SPLIT))
-        for t in range(2):
-            nc.vector.tensor_copy(picked[:, t, :], planes[t][:].indirect(offs_sb[:]))
+        def gather_scalar(t):
+            nc.scalar.activation(grouped[:, SPLIT:S, t], rounded[t][:].indirect(offs_sb[:, SPLIT // 16 : S // 16]), COPY)
+
+        gather_vector(2, (0, SPLIT))
+        gather_scalar(2)
+        nc.vector.tensor_copy(picked[:, 0, :], planes[0][:].indirect(offs_sb[:]))
         for h in range(2):
+            nc.vector.tensor_copy(picked[:, 1, half_cols(h)], planes[1][:].indirect(half_list(offs_sb, h)))
             nc.scalar.copy(grouped[:, half_cols(h), 0:2], picked[:, :, half_cols(h)].rearrange("p t n -> p n t"))
         nc.vector.tensor_copy(old[0][:], store[0][:].indirect(slot_sb[:]))
-        gather_shared(3, (0, HALF, SPLIT))
+        gather_vector(3, (0, FIRST, SPLIT))
 
         codes = keep.tile([P, S], U32, name="codes", align_bytes=64)
         scales = keep.tile([P, S], U8, name="scales", align_bytes=64)
         gate = [keep.tile([P, S], F32, name="gate%d" % b) for b in range(2)]
-        acc = [[psum.tile([P, HALF], F32, name="acc%d_%d" % (b, h)) for h in range(2)] for b in range(2)]
 
-        def gates(h):
-            cols = half_cols(h)
+        def quantise(lo, hi):
             nc.vector.quantize_mx(
-                out=codes[:, cols].bitcast(FP8X4),
-                scales=scales[:, cols],
-                in_=grouped[:, cols, :].rearrange("p n t -> p (n t)"),
+                out=codes[:, lo:hi].bitcast(FP8X4),
+                scales=scales[:, lo:hi],
+                in_=grouped[:, lo:hi, :].rearrange("p n t -> p (n t)"),
             )
-            for b in range(2):
+
+        def gates(b, cuts):
+            first, last = cuts[0], cuts[-1]
+            acc = psum.tile([P, last - first], F32, name="acc%d_%d" % (b, first))
+            for lo, hi in zip(cuts, cuts[1:]):
                 nc.tensor.matmul_mx(
-                    out=acc[b][h][:],
+                    out=acc[:, lo - first : hi - first],
                     lhsT=w_words[:, b * P : (b + 1) * P].bitcast(FP8X4),
                     lhsT_scale=w_scales[:, b * P : (b + 1) * P],
-                    rhs=codes[:, cols].bitcast(FP8X4),
-                    rhs_scale=scales[:, cols],
+                    rhs=codes[:, lo:hi].bitcast(FP8X4),
+                    rhs_scale=scales[:, lo:hi],
                     start=True,
                     stop=True,
                 )
-                nc.scalar.activation(gate[b][:, cols], acc[b][h][:], SIGMOID)
+            nc.scalar.activation(gate[b][:, first:last], acc[:], SIGMOID)
 
-        def put(b, h):
+        def put(b, lo, hi):
             nc.vector.tensor_tensor(
-                store[b][:].indirect(half_list(slot_sb, h)), old[b][:, half_cols(h)], gate[b][:, half_cols(h)], MULT
+                store[b][:].indirect(slot_sb[:, lo // 16 : hi // 16]), old[b][:, lo:hi], gate[b][:, lo:hi], MULT
             )
 
-        gates(0)
+        quantise(0, FIRST)
+        gates(0, (0, FIRST))
+        quantise(FIRST, HALF)
+        gather_scalar(3)
+        gates(1, (0, HALF))
         nc.vector.tensor_copy(old[1][:], store[1][:].indirect(slot_sb[:]))
-        put(0, 0)
-        gates(1)
-        put(1, 0)
-        for b in range(2):
-            put(b, 1)
-            nc.sync.dma_start(out[b * P : (b + 1) * P, :], store[b][:])
+        put(0, 0, FIRST)
+        quantise(HALF, S)
+        gates(0, (FIRST, HALF, S))
+        gates(1, (HALF, S))
+        put(1, 0, HALF)
+        put(0, FIRST, S)
+        nc.sync.dma_start(out[0:P, :], store[0][:])
+        put(1, HALF, S)
+        nc.sync.dma_start(out[P : 2 * P, :], store[1][:])

@@ -19,9 +19,9 @@ MULT = mybir.AluOpType.mult
 P = 128
 PACK = 4
 HALF = S // 2
-SPLIT = 256
-FIRST = 128
 LIST_COLS = S // 16
+SPLIT = 320
+FIRST = 128
 
 
 def tile_picked_idxput_gate_e_kernel(tc, xT, mem, w1_words, w1_scales, offs, slot, out):
@@ -40,51 +40,37 @@ def tile_picked_idxput_gate_e_kernel(tc, xT, mem, w1_words, w1_scales, offs, slo
         x_rows = xT.rearrange("(p t) c -> p t c", t=PACK)
         w_rows = w1_words[0].rearrange("p n t -> p (n t)").bitcast(I32)
         nc.vector.memset(w_scales[:].bitcast(I32), 0)
-        nc.sync.dma_start(planes[2][:], x_rows[:, 2, :])
-        nc.sync.dma_start(offs_sb[:], offs)
         nc.sync.dma_start(planes[0][:], x_rows[:, 0, :])
+        nc.sync.dma_start(offs_sb[:], offs)
+        nc.sync.dma_start(planes[1][:], x_rows[:, 1, :])
         for q in range(4):
             nc.sync.dma_start(w_scales[32 * q : 32 * q + 4, :].bitcast(I32), w1_scales[0, 4 * q : 4 * q + 4, :].bitcast(I32))
-        nc.sync.dma_start(planes[1][:], x_rows[:, 1, :])
+        nc.sync.dma_start(planes[2][:], x_rows[:, 2, :])
         nc.sync.dma_start(slot_sb[:], slot)
-        nc.sync.dma_start(store[0][:], mem[0:P, :])
-        nc.sync.dma_start(w_words[:, 0:P].bitcast(I32), w_rows[:, 0:P])
         nc.sync.dma_start(planes[3][:], x_rows[:, 3, :])
+        nc.sync.dma_start(store[0][:], mem[0:P, :])
+        nc.sync.dma_start(w_words[:].bitcast(I32), w_rows)
         nc.sync.dma_start(store[1][:], mem[P : 2 * P, :])
-        nc.sync.dma_start(w_words[:, P : 2 * P].bitcast(I32), w_rows[:, P : 2 * P])
 
         warm = keep.tile([P, 2], F32, name="warm")
         nc.vector.memset(warm[:, 0:1], 0.0)
         nc.scalar.activation(warm[:, 1:2], warm[:, 0:1], SIGMOID)
 
-        def half_cols(h):
-            return slice(h * HALF, (h + 1) * HALF)
-
-        def half_list(tile, h):
-            return tile[:, h * LIST_COLS // 2 : (h + 1) * LIST_COLS // 2]
+        def entries(tile, lo, hi):
+            return tile[:, lo // 16 : hi // 16]
 
         old = [keep.tile([P, S], F32, name="old%d" % b) for b in range(2)]
+        new = keep.tile([P, S], F32, name="new")
         grouped = keep.tile([P, S, PACK], BF16, name="grouped", align_bytes=64)
-        picked = keep.tile([P, 2, S], BF16, name="picked")
+        picked = keep.tile([P, PACK, S - SPLIT], BF16, name="picked")
 
-        rounded = {t: keep.tile([P, T], BF16, name="rounded%d" % t) for t in (2, 3)}
-
-        def gather_vector(t, cuts):
+        for t in range(PACK):
+            cuts = (0, FIRST, SPLIT) if t == PACK - 1 else (0, SPLIT)
             for lo, hi in zip(cuts, cuts[1:]):
-                nc.vector.tensor_copy(grouped[:, lo:hi, t], planes[t][:].indirect(offs_sb[:, lo // 16 : hi // 16]))
-            nc.scalar.copy(rounded[t][:], planes[t][:])
-
-        def gather_scalar(t):
-            nc.scalar.activation(grouped[:, SPLIT:S, t], rounded[t][:].indirect(offs_sb[:, SPLIT // 16 : S // 16]), COPY)
-
-        gather_vector(2, (0, SPLIT))
-        gather_scalar(2)
-        nc.vector.tensor_copy(picked[:, 0, :], planes[0][:].indirect(offs_sb[:]))
-        for h in range(2):
-            nc.vector.tensor_copy(picked[:, 1, half_cols(h)], planes[1][:].indirect(half_list(offs_sb, h)))
-            nc.scalar.copy(grouped[:, half_cols(h), 0:2], picked[:, :, half_cols(h)].rearrange("p t n -> p n t"))
-        nc.vector.tensor_copy(old[0][:], store[0][:].indirect(slot_sb[:]))
-        gather_vector(3, (0, FIRST, SPLIT))
+                nc.vector.tensor_copy(grouped[:, lo:hi, t], planes[t][:].indirect(entries(offs_sb, lo, hi)))
+            nc.scalar.activation(picked[:, t, :], planes[t][:].indirect(entries(offs_sb, SPLIT, S)), COPY)
+            if t % 2 == 1:
+                nc.scalar.copy(grouped[:, SPLIT:S, t - 1 : t + 1], picked[:, t - 1 : t + 1, :].rearrange("p t n -> p n t"))
 
         codes = keep.tile([P, S], U32, name="codes", align_bytes=64)
         scales = keep.tile([P, S], U8, name="scales", align_bytes=64)
@@ -97,38 +83,33 @@ def tile_picked_idxput_gate_e_kernel(tc, xT, mem, w1_words, w1_scales, offs, slo
                 in_=grouped[:, lo:hi, :].rearrange("p n t -> p (n t)"),
             )
 
-        def gates(b, cuts):
-            first, last = cuts[0], cuts[-1]
-            acc = psum.tile([P, last - first], F32, name="acc%d_%d" % (b, first))
-            for lo, hi in zip(cuts, cuts[1:]):
-                nc.tensor.matmul_mx(
-                    out=acc[:, lo - first : hi - first],
-                    lhsT=w_words[:, b * P : (b + 1) * P].bitcast(FP8X4),
-                    lhsT_scale=w_scales[:, b * P : (b + 1) * P],
-                    rhs=codes[:, lo:hi].bitcast(FP8X4),
-                    rhs_scale=scales[:, lo:hi],
-                    start=True,
-                    stop=True,
-                )
-            nc.scalar.activation(gate[b][:, first:last], acc[:], SIGMOID)
-
-        def put(b, lo, hi):
-            nc.vector.tensor_tensor(
-                store[b][:].indirect(slot_sb[:, lo // 16 : hi // 16]), old[b][:, lo:hi], gate[b][:, lo:hi], MULT
+        def gates(b, lo, hi):
+            acc = psum.tile([P, hi - lo], F32, name="acc%d_%d" % (b, lo))
+            nc.tensor.matmul_mx(
+                out=acc[:],
+                lhsT=w_words[:, b * P : (b + 1) * P].bitcast(FP8X4),
+                lhsT_scale=w_scales[:, b * P : (b + 1) * P],
+                rhs=codes[:, lo:hi].bitcast(FP8X4),
+                rhs_scale=scales[:, lo:hi],
+                start=True,
+                stop=True,
             )
+            nc.scalar.activation(gate[b][:, lo:hi], acc[:], SIGMOID)
 
         quantise(0, FIRST)
-        gates(0, (0, FIRST))
         quantise(FIRST, HALF)
-        gather_scalar(3)
-        gates(1, (0, HALF))
-        nc.vector.tensor_copy(old[1][:], store[1][:].indirect(slot_sb[:]))
-        put(0, 0, FIRST)
         quantise(HALF, S)
-        gates(0, (FIRST, HALF, S))
-        gates(1, (HALF, S))
-        put(1, 0, HALF)
-        put(0, FIRST, S)
+        nc.scalar.activation(old[0][:, HALF:S], store[0][:].indirect(entries(slot_sb, HALF, S)), COPY)
+        nc.vector.tensor_copy(old[0][:, 0:HALF], store[0][:].indirect(entries(slot_sb, 0, HALF)))
+        gates(0, 0, HALF)
+        gates(0, HALF, S)
+        nc.vector.tensor_tensor(new[:, 0:HALF], old[0][:, 0:HALF], gate[0][:, 0:HALF], MULT)
+        gates(1, 0, HALF)
+        nc.scalar.activation(store[0][:].indirect(entries(slot_sb, 0, HALF)), new[:, 0:HALF], COPY)
+        nc.vector.tensor_copy(old[1][:], store[1][:].indirect(slot_sb[:]))
+        nc.vector.tensor_tensor(new[:, HALF:S], old[0][:, HALF:S], gate[0][:, HALF:S], MULT)
+        gates(1, HALF, S)
+        nc.scalar.activation(store[0][:].indirect(entries(slot_sb, HALF, S)), new[:, HALF:S], COPY)
         nc.sync.dma_start(out[0:P, :], store[0][:])
-        put(1, HALF, S)
+        nc.vector.tensor_tensor(store[1][:].indirect(slot_sb[:]), old[1][:], gate[1][:], MULT)
         nc.sync.dma_start(out[P : 2 * P, :], store[1][:])

@@ -43,12 +43,12 @@ def tile_picked_idxput_gate_e_kernel(tc, xT, mem, w1_words, w1_scales, offs, slo
         nc.sync.dma_start(planes[0][:], x_rows[:, 0, :])
         nc.sync.dma_start(offs_sb[:], offs)
         nc.sync.dma_start(planes[1][:], x_rows[:, 1, :])
+        nc.sync.dma_start(planes[2][:], x_rows[:, 2, :])
+        nc.sync.dma_start(planes[3][:], x_rows[:, 3, :])
+        nc.sync.dma_start(slot_sb[:], slot)
+        nc.sync.dma_start(store[0][:], mem[0:P, :])
         for q in range(4):
             nc.sync.dma_start(w_scales[32 * q : 32 * q + 4, :].bitcast(I32), w1_scales[0, 4 * q : 4 * q + 4, :].bitcast(I32))
-        nc.sync.dma_start(planes[2][:], x_rows[:, 2, :])
-        nc.sync.dma_start(slot_sb[:], slot)
-        nc.sync.dma_start(planes[3][:], x_rows[:, 3, :])
-        nc.sync.dma_start(store[0][:], mem[0:P, :])
         nc.sync.dma_start(w_words[:].bitcast(I32), w_rows)
         nc.sync.dma_start(store[1][:], mem[P : 2 * P, :])
 
@@ -99,16 +99,16 @@ def tile_picked_idxput_gate_e_kernel(tc, xT, mem, w1_words, w1_scales, offs, slo
         quantise(0, FIRST)
         quantise(FIRST, HALF)
         quantise(HALF, S)
-        nc.scalar.activation(old[0][:, HALF:S], store[0][:].indirect(entries(slot_sb, HALF, S)), COPY)
-        nc.vector.tensor_copy(old[0][:, 0:HALF], store[0][:].indirect(entries(slot_sb, 0, HALF)))
+        nc.scalar.activation(old[0][:, 0:HALF], store[0][:].indirect(entries(slot_sb, 0, HALF)), COPY)
+        nc.vector.tensor_copy(old[0][:, HALF:S], store[0][:].indirect(entries(slot_sb, HALF, S)))
         gates(0, 0, HALF)
-        gates(0, HALF, S)
         nc.vector.tensor_tensor(new[:, 0:HALF], old[0][:, 0:HALF], gate[0][:, 0:HALF], MULT)
         gates(1, 0, HALF)
+        gates(1, HALF, S)
+        gates(0, HALF, S)
         nc.scalar.activation(store[0][:].indirect(entries(slot_sb, 0, HALF)), new[:, 0:HALF], COPY)
         nc.vector.tensor_copy(old[1][:], store[1][:].indirect(slot_sb[:]))
         nc.vector.tensor_tensor(new[:, HALF:S], old[0][:, HALF:S], gate[0][:, HALF:S], MULT)
-        gates(1, HALF, S)
         nc.scalar.activation(store[0][:].indirect(entries(slot_sb, HALF, S)), new[:, HALF:S], COPY)
         nc.sync.dma_start(out[0:P, :], store[0][:])
         nc.vector.tensor_tensor(store[1][:].indirect(slot_sb[:]), old[1][:], gate[1][:], MULT)

@@ -22,6 +22,7 @@ HALF = S // 2
 LIST_COLS = S // 16
 SPLIT = 320
 FIRST = 128
+SHARE0 = 256
 
 
 def tile_picked_idxput_gate_e_kernel(tc, xT, mem, w1_words, w1_scales, offs, slot, out):
@@ -62,15 +63,18 @@ def tile_picked_idxput_gate_e_kernel(tc, xT, mem, w1_words, w1_scales, offs, slo
         old = [keep.tile([P, S], F32, name="old%d" % b) for b in range(2)]
         new = keep.tile([P, S], F32, name="new")
         grouped = keep.tile([P, S, PACK], BF16, name="grouped", align_bytes=64)
-        picked = keep.tile([P, PACK, S - SPLIT], BF16, name="picked")
+        middle = S - FIRST
+        picked = {lo: keep.tile([P, PACK, hi - lo], BF16, name="picked%d" % lo) for lo, hi in ((SPLIT, middle), (middle, S))}
 
         for t in range(PACK):
             cuts = (0, FIRST, SPLIT) if t == PACK - 1 else (0, SPLIT)
             for lo, hi in zip(cuts, cuts[1:]):
                 nc.vector.tensor_copy(grouped[:, lo:hi, t], planes[t][:].indirect(entries(offs_sb, lo, hi)))
-            nc.scalar.activation(picked[:, t, :], planes[t][:].indirect(entries(offs_sb, SPLIT, S)), COPY)
+            for lo, hi in ((SPLIT, middle), (middle, S)):
+                nc.scalar.activation(picked[lo][:, t, :], planes[t][:].indirect(entries(offs_sb, lo, hi)), COPY)
             if t % 2 == 1:
-                nc.scalar.copy(grouped[:, SPLIT:S, t - 1 : t + 1], picked[:, t - 1 : t + 1, :].rearrange("p t n -> p n t"))
+                for lo, hi in ((SPLIT, middle), (middle, S)):
+                    nc.scalar.copy(grouped[:, lo:hi, t - 1 : t + 1], picked[lo][:, t - 1 : t + 1, :].rearrange("p t n -> p n t"))
 
         codes = keep.tile([P, S], U32, name="codes", align_bytes=64)
         scales = keep.tile([P, S], U8, name="scales", align_bytes=64)
@@ -98,9 +102,10 @@ def tile_picked_idxput_gate_e_kernel(tc, xT, mem, w1_words, w1_scales, offs, slo
 
         quantise(0, FIRST)
         quantise(FIRST, HALF)
-        quantise(HALF, S)
-        nc.scalar.activation(old[0][:, 0:HALF], store[0][:].indirect(entries(slot_sb, 0, HALF)), COPY)
-        nc.vector.tensor_copy(old[0][:, HALF:S], store[0][:].indirect(entries(slot_sb, HALF, S)))
+        quantise(HALF, middle)
+        quantise(middle, S)
+        nc.scalar.activation(old[0][:, 0:SHARE0], store[0][:].indirect(entries(slot_sb, 0, SHARE0)), COPY)
+        nc.vector.tensor_copy(old[0][:, SHARE0:S], store[0][:].indirect(entries(slot_sb, SHARE0, S)))
         gates(0, 0, HALF)
         nc.vector.tensor_tensor(new[:, 0:HALF], old[0][:, 0:HALF], gate[0][:, 0:HALF], MULT)
         gates(1, 0, HALF)

@@ -20,7 +20,7 @@ P = 128
 PACK = 4
 HALF = S // 2
 LIST_COLS = S // 16
-SPLIT = 320
+SPLIT = 288
 FIRST = 128
 SHARE0 = 256
 
@@ -40,7 +40,6 @@ def tile_picked_idxput_gate_e_kernel(tc, xT, mem, w1_words, w1_scales, offs, slo
 
         x_rows = xT.rearrange("(p t) c -> p t c", t=PACK)
         w_rows = w1_words[0].rearrange("p n t -> p (n t)").bitcast(I32)
-        nc.vector.memset(w_scales[:].bitcast(I32), 0)
         nc.sync.dma_start(planes[0][:], x_rows[:, 0, :])
         nc.sync.dma_start(offs_sb[:], offs)
         nc.sync.dma_start(planes[1][:], x_rows[:, 1, :])

@@ -40,6 +40,8 @@ def tile_picked_idxput_gate_e_kernel(tc, xT, mem, w1_words, w1_scales, offs, slo
 
         x_rows = xT.rearrange("(p t) c -> p t c", t=PACK)
         w_rows = w1_words[0].rearrange("p n t -> p (n t)").bitcast(I32)
+        for q in range(4):
+            nc.scalar.dma_start(w_scales[32 * q : 32 * q + 4, :].bitcast(I32), w1_scales[0, 4 * q : 4 * q + 4, :].bitcast(I32))
         nc.sync.dma_start(planes[0][:], x_rows[:, 0, :])
         nc.sync.dma_start(offs_sb[:], offs)
         nc.sync.dma_start(planes[1][:], x_rows[:, 1, :])
@@ -47,8 +49,6 @@ def tile_picked_idxput_gate_e_kernel(tc, xT, mem, w1_words, w1_scales, offs, slo
         nc.sync.dma_start(planes[3][:], x_rows[:, 3, :])
         nc.sync.dma_start(slot_sb[:], slot)
         nc.sync.dma_start(store[0][:], mem[0:P, :])
-        for q in range(4):
-            nc.sync.dma_start(w_scales[32 * q : 32 * q + 4, :].bitcast(I32), w1_scales[0, 4 * q : 4 * q + 4, :].bitcast(I32))
         nc.sync.dma_start(w_words[:].bitcast(I32), w_rows)
         nc.sync.dma_start(store[1][:], mem[P : 2 * P, :])
 
@@ -63,17 +63,27 @@ def tile_picked_idxput_gate_e_kernel(tc, xT, mem, w1_words, w1_scales, offs, slo
         new = keep.tile([P, S], F32, name="new")
         grouped = keep.tile([P, S, PACK], BF16, name="grouped", align_bytes=64)
         middle = S - FIRST
-        picked = {lo: keep.tile([P, PACK, hi - lo], BF16, name="picked%d" % lo) for lo, hi in ((SPLIT, middle), (middle, S))}
+        shares = {0: (SPLIT, middle, S), 1: (HALF, middle, S)}
+        rows = {
+            (u, lo): keep.tile([P, 2, hi - lo], BF16, name="rows%d_%d" % (u, lo))
+            for u, cuts in shares.items()
+            for lo, hi in zip(cuts, cuts[1:])
+        }
+
+        def woven(u, lo, hi):
+            return grouped[:, lo:hi, 2 * u : 2 * u + 2], rows[u, lo][:].rearrange("p t n -> p n t")
 
         for t in range(PACK):
-            cuts = (0, FIRST, SPLIT) if t == PACK - 1 else (0, SPLIT)
+            share = shares[t // 2]
+            cuts = (0, FIRST, share[0]) if t == PACK - 1 else (0, share[0])
             for lo, hi in zip(cuts, cuts[1:]):
                 nc.vector.tensor_copy(grouped[:, lo:hi, t], planes[t][:].indirect(entries(offs_sb, lo, hi)))
-            for lo, hi in ((SPLIT, middle), (middle, S)):
-                nc.scalar.activation(picked[lo][:, t, :], planes[t][:].indirect(entries(offs_sb, lo, hi)), COPY)
-            if t % 2 == 1:
-                for lo, hi in ((SPLIT, middle), (middle, S)):
-                    nc.scalar.copy(grouped[:, lo:hi, t - 1 : t + 1], picked[lo][:, t - 1 : t + 1, :].rearrange("p t n -> p n t"))
+            for lo, hi in zip(share, share[1:]):
+                nc.scalar.activation(rows[t // 2, lo][:, t % 2, :], planes[t][:].indirect(entries(offs_sb, lo, hi)), COPY)
+            if t == 1:
+                for lo, hi in zip(share, share[1:]):
+                    nc.scalar.copy(*woven(0, lo, hi))
+        nc.scalar.copy(*woven(1, HALF, middle))
 
         codes = keep.tile([P, S], U32, name="codes", align_bytes=64)
         scales = keep.tile([P, S], U8, name="scales", align_bytes=64)
@@ -101,6 +111,7 @@ def tile_picked_idxput_gate_e_kernel(tc, xT, mem, w1_words, w1_scales, offs, slo
 
         quantise(0, FIRST)
         quantise(FIRST, HALF)
+        nc.vector.tensor_copy(*woven(1, middle, S))
         quantise(HALF, middle)
         quantise(middle, S)
         nc.scalar.activation(old[0][:, 0:SHARE0], store[0][:].indirect(entries(slot_sb, 0, SHARE0)), COPY)

@@ -116,7 +116,8 @@ def tile_picked_idxput_gate_e_kernel(tc, xT, mem, w1_words, w1_scales, offs, slo
         quantise(middle, S)
         nc.scalar.activation(old[0][:, 0:SHARE0], store[0][:].indirect(entries(slot_sb, 0, SHARE0)), COPY)
         nc.vector.tensor_copy(old[0][:, SHARE0:S], store[0][:].indirect(entries(slot_sb, SHARE0, S)))
-        gates(0, 0, HALF)
+        gates(0, 0, FIRST)
+        gates(0, FIRST, HALF)
         nc.vector.tensor_tensor(new[:, 0:HALF], old[0][:, 0:HALF], gate[0][:, 0:HALF], MULT)
         gates(1, 0, HALF)
         gates(1, HALF, S)

@@ -22,7 +22,7 @@ HALF = S // 2
 LIST_COLS = S // 16
 SPLIT = 288
 FIRST = 128
-SHARE0 = 256
+SHARE0 = 352
 
 
 def tile_picked_idxput_gate_e_kernel(tc, xT, mem, w1_words, w1_scales, offs, slot, out):

@@ -22,7 +22,8 @@ HALF = S // 2
 LIST_COLS = S // 16
 SPLIT = 288
 FIRST = 128
-SHARE0 = 352
+SHARE0 = 384
+SHARE1 = 384
 
 
 def tile_picked_idxput_gate_e_kernel(tc, xT, mem, w1_words, w1_scales, offs, slot, out):
@@ -117,15 +118,15 @@ def tile_picked_idxput_gate_e_kernel(tc, xT, mem, w1_words, w1_scales, offs, slo
         nc.scalar.activation(old[0][:, 0:SHARE0], store[0][:].indirect(entries(slot_sb, 0, SHARE0)), COPY)
         nc.vector.tensor_copy(old[0][:, SHARE0:S], store[0][:].indirect(entries(slot_sb, SHARE0, S)))
         gates(0, 0, FIRST)
+        nc.vector.tensor_tensor(store[0][:].indirect(entries(slot_sb, 0, FIRST)), old[0][:, 0:FIRST], gate[0][:, 0:FIRST], MULT)
         gates(0, FIRST, HALF)
-        nc.vector.tensor_tensor(new[:, 0:HALF], old[0][:, 0:HALF], gate[0][:, 0:HALF], MULT)
         gates(1, 0, HALF)
-        gates(1, HALF, S)
         gates(0, HALF, S)
-        nc.scalar.activation(store[0][:].indirect(entries(slot_sb, 0, HALF)), new[:, 0:HALF], COPY)
-        nc.vector.tensor_copy(old[1][:], store[1][:].indirect(slot_sb[:]))
-        nc.vector.tensor_tensor(new[:, HALF:S], old[0][:, HALF:S], gate[0][:, HALF:S], MULT)
-        nc.scalar.activation(store[0][:].indirect(entries(slot_sb, HALF, S)), new[:, HALF:S], COPY)
+        gates(1, HALF, S)
+        nc.vector.tensor_tensor(new[:, FIRST:S], old[0][:, FIRST:S], gate[0][:, FIRST:S], MULT)
+        nc.scalar.activation(old[1][:, 0:SHARE1], store[1][:].indirect(entries(slot_sb, 0, SHARE1)), COPY)
+        nc.vector.tensor_copy(old[1][:, SHARE1:S], store[1][:].indirect(entries(slot_sb, SHARE1, S)))
+        nc.scalar.activation(store[0][:].indirect(entries(slot_sb, FIRST, S)), new[:, FIRST:S], COPY)
         nc.sync.dma_start(out[0:P, :], store[0][:])
         nc.vector.tensor_tensor(store[1][:].indirect(slot_sb[:]), old[1][:], gate[1][:], MULT)
         nc.sync.dma_start(out[P : 2 * P, :], store[1][:])

@@ -20,8 +20,7 @@ P = 128
 PACK = 4
 HALF = S // 2
 LIST_COLS = S // 16
-SPLIT = 288
-FIRST = 128
+PIECE = 128
 SHARE0 = 384
 SHARE1 = 384
 
@@ -45,9 +44,8 @@ def tile_picked_idxput_gate_e_kernel(tc, xT, mem, w1_words, w1_scales, offs, slo
             nc.scalar.dma_start(w_scales[32 * q : 32 * q + 4, :].bitcast(I32), w1_scales[0, 4 * q : 4 * q + 4, :].bitcast(I32))
         nc.sync.dma_start(planes[0][:], x_rows[:, 0, :])
         nc.sync.dma_start(offs_sb[:], offs)
-        nc.sync.dma_start(planes[1][:], x_rows[:, 1, :])
-        nc.sync.dma_start(planes[2][:], x_rows[:, 2, :])
-        nc.sync.dma_start(planes[3][:], x_rows[:, 3, :])
+        for t in range(1, PACK):
+            nc.sync.dma_start(planes[t][:], x_rows[:, t, :])
         nc.sync.dma_start(slot_sb[:], slot)
         nc.sync.dma_start(store[0][:], mem[0:P, :])
         nc.sync.dma_start(w_words[:].bitcast(I32), w_rows)
@@ -60,42 +58,26 @@ def tile_picked_idxput_gate_e_kernel(tc, xT, mem, w1_words, w1_scales, offs, slo
         def entries(tile, lo, hi):
             return tile[:, lo // 16 : hi // 16]
 
-        old = [keep.tile([P, S], F32, name="old%d" % b) for b in range(2)]
-        new = keep.tile([P, S], F32, name="new")
         grouped = keep.tile([P, S, PACK], BF16, name="grouped", align_bytes=64)
-        middle = S - FIRST
-        shares = {0: (SPLIT, middle, S), 1: (HALF, middle, S)}
-        rows = {
-            (u, lo): keep.tile([P, 2, hi - lo], BF16, name="rows%d_%d" % (u, lo))
-            for u, cuts in shares.items()
-            for lo, hi in zip(cuts, cuts[1:])
-        }
-
-        def woven(u, lo, hi):
-            return grouped[:, lo:hi, 2 * u : 2 * u + 2], rows[u, lo][:].rearrange("p t n -> p n t")
-
         for t in range(PACK):
-            share = shares[t // 2]
-            cuts = (0, FIRST, share[0]) if t == PACK - 1 else (0, share[0])
-            for lo, hi in zip(cuts, cuts[1:]):
-                nc.vector.tensor_copy(grouped[:, lo:hi, t], planes[t][:].indirect(entries(offs_sb, lo, hi)))
-            for lo, hi in zip(share, share[1:]):
-                nc.scalar.activation(rows[t // 2, lo][:, t % 2, :], planes[t][:].indirect(entries(offs_sb, lo, hi)), COPY)
-            if t == 1:
-                for lo, hi in zip(share, share[1:]):
-                    nc.scalar.copy(*woven(0, lo, hi))
-        nc.scalar.copy(*woven(1, HALF, middle))
+            step = PIECE if t == PACK - 1 else HALF
+            for lo in range(0, HALF, step):
+                nc.vector.tensor_copy(grouped[:, lo : lo + step, t], planes[t][:].indirect(entries(offs_sb, lo, lo + step)))
+            for lo in range(HALF, S, step):
+                nc.scalar.activation(grouped[:, lo : lo + step, t], planes[t][:].indirect(entries(offs_sb, lo, lo + step)), COPY)
 
         codes = keep.tile([P, S], U32, name="codes", align_bytes=64)
         scales = keep.tile([P, S], U8, name="scales", align_bytes=64)
-        gate = [keep.tile([P, S], F32, name="gate%d" % b) for b in range(2)]
-
-        def quantise(lo, hi):
+        for lo in (0, 2 * PIECE, PIECE, 3 * PIECE):
             nc.vector.quantize_mx(
-                out=codes[:, lo:hi].bitcast(FP8X4),
-                scales=scales[:, lo:hi],
-                in_=grouped[:, lo:hi, :].rearrange("p n t -> p (n t)"),
+                out=codes[:, lo : lo + PIECE].bitcast(FP8X4),
+                scales=scales[:, lo : lo + PIECE],
+                in_=grouped[:, lo : lo + PIECE, :].rearrange("p n t -> p (n t)"),
             )
+
+        old = [keep.tile([P, S], F32, name="old%d" % b) for b in range(2)]
+        gate = [keep.tile([P, S], F32, name="gate%d" % b) for b in range(2)]
+        new = keep.tile([P, S], F32, name="new")
 
         def gates(b, lo, hi):
             acc = psum.tile([P, hi - lo], F32, name="acc%d_%d" % (b, lo))
@@ -110,23 +92,20 @@ def tile_picked_idxput_gate_e_kernel(tc, xT, mem, w1_words, w1_scales, offs, slo
             )
             nc.scalar.activation(gate[b][:, lo:hi], acc[:], SIGMOID)
 
-        quantise(0, FIRST)
-        quantise(FIRST, HALF)
-        nc.vector.tensor_copy(*woven(1, middle, S))
-        quantise(HALF, middle)
-        quantise(middle, S)
-        nc.scalar.activation(old[0][:, 0:SHARE0], store[0][:].indirect(entries(slot_sb, 0, SHARE0)), COPY)
-        nc.vector.tensor_copy(old[0][:, SHARE0:S], store[0][:].indirect(entries(slot_sb, SHARE0, S)))
-        gates(0, 0, FIRST)
-        nc.vector.tensor_tensor(store[0][:].indirect(entries(slot_sb, 0, FIRST)), old[0][:, 0:FIRST], gate[0][:, 0:FIRST], MULT)
-        gates(0, FIRST, HALF)
+        def look_up(b, share):
+            nc.scalar.activation(old[b][:, 0:share], store[b][:].indirect(entries(slot_sb, 0, share)), COPY)
+            nc.vector.tensor_copy(old[b][:, share:S], store[b][:].indirect(entries(slot_sb, share, S)))
+
+        look_up(0, SHARE0)
+        gates(0, 0, PIECE)
+        nc.vector.tensor_tensor(store[0][:].indirect(entries(slot_sb, 0, PIECE)), old[0][:, 0:PIECE], gate[0][:, 0:PIECE], MULT)
+        gates(0, PIECE, HALF)
         gates(1, 0, HALF)
         gates(0, HALF, S)
         gates(1, HALF, S)
-        nc.vector.tensor_tensor(new[:, FIRST:S], old[0][:, FIRST:S], gate[0][:, FIRST:S], MULT)
-        nc.scalar.activation(old[1][:, 0:SHARE1], store[1][:].indirect(entries(slot_sb, 0, SHARE1)), COPY)
-        nc.vector.tensor_copy(old[1][:, SHARE1:S], store[1][:].indirect(entries(slot_sb, SHARE1, S)))
-        nc.scalar.activation(store[0][:].indirect(entries(slot_sb, FIRST, S)), new[:, FIRST:S], COPY)
+        nc.vector.tensor_tensor(new[:, PIECE:S], old[0][:, PIECE:S], gate[0][:, PIECE:S], MULT)
+        look_up(1, SHARE1)
+        nc.scalar.activation(store[0][:].indirect(entries(slot_sb, PIECE, S)), new[:, PIECE:S], COPY)
         nc.sync.dma_start(out[0:P, :], store[0][:])
         nc.vector.tensor_tensor(store[1][:].indirect(slot_sb[:]), old[1][:], gate[1][:], MULT)
         nc.sync.dma_start(out[P : 2 * P, :], store[1][:])

@@ -21,7 +21,7 @@ PACK = 4
 HALF = S // 2
 LIST_COLS = S // 16
 PIECE = 128
-SHARE0 = 384
+SHARE0 = 320
 SHARE1 = 384
 
 

@@ -21,7 +21,7 @@ PACK = 4
 HALF = S // 2
 LIST_COLS = S // 16
 PIECE = 128
-SHARE0 = 320
+SHARE0 = 256
 SHARE1 = 384
 
 

from contextlib import ExitStack

import concourse.mybir as mybir

K, T, S, N, U = 512, 1024, 512, 256, 1024
FLOPS = 2 * K * N * S

F32 = mybir.dt.float32
BF16 = mybir.dt.bfloat16
I32 = mybir.dt.int32
U32 = mybir.dt.uint32
U16 = mybir.dt.uint16
U8 = mybir.dt.uint8
FP8X4 = mybir.dt.float8_e4m3fn_x4
SIGMOID = mybir.ActivationFunctionType.Sigmoid
COPY = mybir.ActivationFunctionType.Copy
MULT = mybir.AluOpType.mult

P = 128
PACK = 4
HALF = S // 2
LIST_COLS = S // 16
PIECE = 128
SHARE0 = 256
SHARE1 = 384


def tile_picked_idxput_gate_e_kernel(tc, xT, mem, w1_words, w1_scales, offs, slot, out):
    nc = tc.nc
    with ExitStack() as ctx:
        keep = ctx.enter_context(tc.tile_pool(name="keep", bufs=1))
        psum = ctx.enter_context(tc.psum_pool(name="psum", bufs=1))

        offs_sb = keep.tile([P, LIST_COLS], U16, name="offs_sb")
        slot_sb = keep.tile([P, LIST_COLS], U16, name="slot_sb")
        planes = [keep.tile([P, T], F32, name="plane%d" % t) for t in range(PACK)]
        store = [keep.tile([P, U], F32, name="store%d" % b) for b in range(2)]
        w_words = keep.tile([P, N], U32, name="w_words", align_bytes=64)
        w_scales = keep.tile([P, N], U8, name="w_scales", align_bytes=64)

        x_rows = xT.rearrange("(p t) c -> p t c", t=PACK)
        w_rows = w1_words[0].rearrange("p n t -> p (n t)").bitcast(I32)
        for q in range(4):
            nc.scalar.dma_start(w_scales[32 * q : 32 * q + 4, :].bitcast(I32), w1_scales[0, 4 * q : 4 * q + 4, :].bitcast(I32))
        nc.sync.dma_start(planes[0][:], x_rows[:, 0, :])
        nc.sync.dma_start(offs_sb[:], offs)
        for t in range(1, PACK):
            nc.sync.dma_start(planes[t][:], x_rows[:, t, :])
        nc.sync.dma_start(slot_sb[:], slot)
        nc.sync.dma_start(store[0][:], mem[0:P, :])
        nc.sync.dma_start(w_words[:].bitcast(I32), w_rows)
        nc.sync.dma_start(store[1][:], mem[P : 2 * P, :])

        warm = keep.tile([P, 2], F32, name="warm")
        nc.vector.memset(warm[:, 0:1], 0.0)
        nc.scalar.activation(warm[:, 1:2], warm[:, 0:1], SIGMOID)

        def entries(tile, lo, hi):
            return tile[:, lo // 16 : hi // 16]

        grouped = keep.tile([P, S, PACK], BF16, name="grouped", align_bytes=64)
        for t in range(PACK):
            step = PIECE if t == PACK - 1 else HALF
            for lo in range(0, HALF, step):
                nc.vector.tensor_copy(grouped[:, lo : lo + step, t], planes[t][:].indirect(entries(offs_sb, lo, lo + step)))
            for lo in range(HALF, S, step):
                nc.scalar.activation(grouped[:, lo : lo + step, t], planes[t][:].indirect(entries(offs_sb, lo, lo + step)), COPY)

        codes = keep.tile([P, S], U32, name="codes", align_bytes=64)
        scales = keep.tile([P, S], U8, name="scales", align_bytes=64)
        for lo in (0, 2 * PIECE, PIECE, 3 * PIECE):
            nc.vector.quantize_mx(
                out=codes[:, lo : lo + PIECE].bitcast(FP8X4),
                scales=scales[:, lo : lo + PIECE],
                in_=grouped[:, lo : lo + PIECE, :].rearrange("p n t -> p (n t)"),
            )

        old = [keep.tile([P, S], F32, name="old%d" % b) for b in range(2)]
        gate = [keep.tile([P, S], F32, name="gate%d" % b) for b in range(2)]
        new = keep.tile([P, S], F32, name="new")

        def gates(b, lo, hi):
            acc = psum.tile([P, hi - lo], F32, name="acc%d_%d" % (b, lo))
            nc.tensor.matmul_mx(
                out=acc[:],
                lhsT=w_words[:, b * P : (b + 1) * P].bitcast(FP8X4),
                lhsT_scale=w_scales[:, b * P : (b + 1) * P],
                rhs=codes[:, lo:hi].bitcast(FP8X4),
                rhs_scale=scales[:, lo:hi],
                start=True,
                stop=True,
            )
            nc.scalar.activation(gate[b][:, lo:hi], acc[:], SIGMOID)

        def look_up(b, share):
            nc.scalar.activation(old[b][:, 0:share], store[b][:].indirect(entries(slot_sb, 0, share)), COPY)
            nc.vector.tensor_copy(old[b][:, share:S], store[b][:].indirect(entries(slot_sb, share, S)))

        look_up(0, SHARE0)
        gates(0, 0, PIECE)
        nc.vector.tensor_tensor(store[0][:].indirect(entries(slot_sb, 0, PIECE)), old[0][:, 0:PIECE], gate[0][:, 0:PIECE], MULT)
        gates(0, PIECE, HALF)
        gates(1, 0, HALF)
        gates(0, HALF, S)
        gates(1, HALF, S)
        nc.vector.tensor_tensor(new[:, PIECE:S], old[0][:, PIECE:S], gate[0][:, PIECE:S], MULT)
        look_up(1, SHARE1)
        nc.scalar.activation(store[0][:].indirect(entries(slot_sb, PIECE, S)), new[:, PIECE:S], COPY)
        nc.sync.dma_start(out[0:P, :], store[0][:])
        nc.vector.tensor_tensor(store[1][:].indirect(slot_sb[:]), old[1][:], gate[1][:], MULT)
        nc.sync.dma_start(out[P : 2 * P, :], store[1][:])
